import numpy as np
import ml_dtypes


def mxq(x, axis, fmt="e4m3"):
    dtype, down = {"e4m3": (ml_dtypes.float8_e4m3fn, 7), "e5m2": (ml_dtypes.float8_e5m2, 14)}[fmt]
    v = np.moveaxis(np.asarray(x, np.float32).astype(ml_dtypes.bfloat16).astype(np.float64), axis, -1)
    blocks = v.reshape(v.shape[:-1] + (-1, 32))
    amax = np.abs(blocks).max(-1, keepdims=True)
    byte = np.maximum(np.where(amax > 0, np.frexp(amax)[1] - 1 + 127, 0) - down, 1)
    scale = np.exp2(byte - 127.0)
    codes = (blocks / scale).astype(np.float32).astype(dtype).astype(np.float64)
    return np.moveaxis((codes * scale).reshape(v.shape), -1, axis)


WIDE = False


def mx_kscale(k):
    if not WIDE:
        return np.ones(k)
    levels = np.array([10, -10, 5, -5, 0])
    if k % 512:
        return np.exp2(np.random.permutation(np.resize(levels, k // 32))).repeat(32)
    a = np.empty((k // 512, 16))
    for p in range(k // 512):
        a[p, :8] = np.random.permutation(np.resize(levels, 8))
        for g in range(8):
            far = levels[np.abs(levels - a[p, g]) >= 10]
            a[p, g + 8] = far[np.random.randint(len(far))]
    return np.exp2(a.ravel()).repeat(32)


def f64(x):
    return np.asarray(x).astype(np.float64)


def striped(idx):
    return np.tile(idx.reshape(-1, 16).T, (8, 1)).astype(np.uint16)


def unstriped(offs):
    return offs[:16].T.reshape(-1).astype(np.int64)


E2M1 = np.array([0.0, 0.5, 1.0, 1.5, 2.0, 3.0, 4.0, 6.0, -0.0, -0.5, -1.0, -1.5, -2.0, -3.0, -4.0, -6.0])


def pack_weight(w, fmt):
    k, n = w.shape
    w = f64(np.asarray(w, np.float32).astype(ml_dtypes.bfloat16)).reshape(k // 32, 32, n)
    amax = np.abs(w).max(1)
    if fmt == "e4m3":
        byte = np.frexp(amax)[1] - 1 + 127 - 7
    else:
        mant, ex = np.frexp(amax / 6.0)
        byte = np.where(mant > 0.5, ex, ex - 1) + 127
    byte = np.clip(np.where(amax > 0, byte, 1), 1, 254)
    scaled = (w * np.exp2(127.0 - byte)[:, None, :]).reshape(k, n).astype(np.float32)
    by_word = np.ascontiguousarray(scaled.reshape(k // 512, 128, 4, n).transpose(0, 1, 3, 2))
    if fmt == "e4m3":
        words = by_word.astype(ml_dtypes.float8_e4m3fn).view(np.uint8)
    else:
        c = by_word.astype(ml_dtypes.float4_e2m1fn).view(np.uint8) & 0xF
        words = (c[..., 0::2] | (c[..., 1::2] << 4)).reshape(k // 512, 128, 2 * n)
    return np.ascontiguousarray(words), np.ascontiguousarray(byte.astype(np.uint8).reshape(k // 512, 16, n))


def unpack_weight(words, scales, fmt):
    g, _, n = scales.shape
    words = np.ascontiguousarray(words).reshape(g, 128, n, -1)
    if fmt == "e4m3":
        vals = words.view(ml_dtypes.float8_e4m3fn).astype(np.float64)
    else:
        nib = np.empty((g, 128, n, 4), np.uint8)
        nib[..., 0::2] = words & 0xF
        nib[..., 1::2] = words >> 4
        vals = E2M1[nib]
    vals = vals * np.repeat(np.exp2(scales.astype(np.float64) - 127.0), 8, axis=1)[..., None]
    return vals.transpose(0, 1, 3, 2).reshape(g * 512, n)


def relu(v):
    return np.maximum(v, 0.0)


K, T, E, C, N = 2560, 1280, 8, 128, 256


def by_expert(wq, xq):
    return np.concatenate([wq[e].T @ xq[:, e * C:(e + 1) * C] for e in range(E)], axis=1)


def setup_inputs():
    n = np.random.standard_normal
    s = mx_kscale(K)[:, None]
    x = pack_weight(n((K, T)) * s, "e4m3")
    return {
        "x_words": x[0],
        "x_scales": x[1],
        "w": (n((E + 1, K, N)) / np.sqrt(K) / s[None]).astype(np.float32),
        "b": (0.3 * n((N, E + 1))).astype(np.float32),
        "gate": np.tile(np.random.uniform(0.2, 1.0, E * C), (N, 1)).astype(np.float32),
        "offs": striped(np.random.permutation(T)[:E * C]),
    }


def reference(x_words, x_scales, w, b, gate, offs):
    idx = unstriped(offs)
    wq = mxq(f64(w), 1, "e4m3")
    xs = unpack_weight(x_words, x_scales, "e4m3")
    ys = relu((wq[E].T @ xs) + f64(b)[:, E:])
    xq = unpack_weight(x_words, x_scales, "e4m3")[:, idx]
    y = by_expert(wq, xq)
    y = relu(y + np.repeat(f64(b)[:, :E], C, axis=1))
    out = ys
    out[:, idx] += f64(gate) * y
    return out

@@ -1,0 +1,201 @@
+from contextlib import ExitStack
+
+import concourse.mybir as mybir
+from concourse.masks import make_identity
+
+K, T, E, C, N = 2560, 1280, 8, 128, 256
+SLOTS = E * C
+FLOPS = 2 * K * N * (SLOTS + T)
+BYTES = K * T + K * T // 32 + (E + 1) * K * N * 4 + N * (E + 1) * 4 + SLOTS * 4 + 128 * (SLOTS // 16) * 2 + N * T * 4
+
+F32 = mybir.dt.float32
+BF16 = mybir.dt.bfloat16
+I32 = mybir.dt.int32
+U32 = mybir.dt.uint32
+U16 = mybir.dt.uint16
+U8 = mybir.dt.uint8
+FP8X4 = mybir.dt.float8_e4m3fn_x4
+ALU = mybir.AluOpType
+ACT = mybir.ActivationFunctionType
+
+P = 128
+PACK = 4
+K_PASS = P * PACK
+PASSES = K // K_PASS
+HALVES = N // P
+PER_COLUMN = 16
+GATHER = 512
+SCATTER = 160
+BANK = 512
+SHARED = E
+TOKEN_PIECES = [(t0, min(t0 + BANK, T)) for t0 in range(0, T, BANK)]
+
+
+def tile_moe_shr_lin_relu_kernel(tc, x_words, x_scales, w, b, gate, offs, out):
+    nc = tc.nc
+    with ExitStack() as ctx:
+        keep = ctx.enter_context(tc.tile_pool(name="keep", bufs=1))
+        raw_pool = ctx.enter_context(tc.tile_pool(name="raw", bufs=6))
+        grouped_pool = ctx.enter_context(tc.tile_pool(name="grouped", bufs=8))
+        psum = ctx.enter_context(tc.psum_pool(name="psum", bufs=1))
+
+        offsets = keep.tile([P, SLOTS // PER_COLUMN], U16, name="offsets")
+        nc.sync.dma_start(offsets[:], offs)
+
+        gate_rows = keep.tile([P, SLOTS // P], F32, name="gate_rows")
+        planes = [keep.tile([P, T], U8, name="plane%d" % i, align_bytes=64) for i in range(2)]
+        for plane in planes:
+            nc.vector.memset(plane[:].bitcast(I32), 0)
+        scale_loads = [(planes[0][32 * q : 32 * q + 16, :], x_scales[0:4, 4 * q : 4 * q + 4, :]) for q in range(4)]
+        scale_loads.extend([(planes[1][32 * q : 32 * q + 4, :], x_scales[4, 4 * q : 4 * q + 4, :]) for q in range(4)])
+        bias = keep.tile([P, HALVES, E + 1], F32, name="bias")
+
+        routed = [keep.tile([P, T], F32, name="routed%d" % h) for h in range(HALVES)]
+        for h in range(HALVES):
+            nc.vector.memset(routed[h][:], 0.0)
+        identity = keep.tile([P, P], F32, name="identity")
+        make_identity(nc, identity[:])
+
+        gate_full = keep.tile([P, SLOTS], F32, name="gate_full")
+        per_bank = BANK // P
+
+        def spread_gate():
+            nc.sync.dma_start(gate_rows[:], gate[0, :].rearrange("(p m) -> p m", p=P))
+            nc.sync.dma_start(bias[:], b.rearrange("(h p) e -> p h e", p=P))
+            for u in range(SLOTS // BANK):
+                turned = psum.tile([P, per_bank, P], F32, name="turned%d" % u, tag="shared%d" % u)
+                for m in range(per_bank):
+                    column = per_bank * u + m
+                    nc.tensor.transpose(turned[:, m, :], gate_rows[:, column : column + 1].to_broadcast([P, P]), identity[:])
+                nc.scalar.activation(
+                    gate_full[:].rearrange("q (p m) -> q p m", p=P)[:, :, per_bank * u : per_bank * (u + 1)],
+                    turned[:].rearrange("q m p -> q p m"),
+                    ACT.Copy,
+                )
+
+        words = [keep.tile([P, T], I32, name="words%d" % o, align_bytes=64) for o in range(PASSES)]
+        chunks = SLOTS // GATHER
+        slot_words = [[keep.tile([P, GATHER], U32, name="slot_words%d_%d" % (o, c), align_bytes=64) for c in range(chunks)] for o in range(PASSES)]
+        slot_planes = [[keep.tile([P, GATHER], U8, name="slot_plane%d_%d" % (i, c), align_bytes=64) for c in range(chunks)] for i in range(2)]
+        y = [keep.tile([P, SLOTS], F32, name="y%d" % h) for h in range(HALVES)]
+
+        def list_part(j0, j1):
+            return offsets[:, j0 // PER_COLUMN : j1 // PER_COLUMN]
+
+        def load_tokens(o):
+            nc.sync.dma_start(words[o][:], x_words[o].rearrange("p t r -> p (t r)").bitcast(I32))
+            for c in range(chunks):
+                nc.vector.tensor_copy(slot_words[o][c][:], words[o][:].bitcast(U32).indirect(list_part(c * GATHER, (c + 1) * GATHER)))
+
+        def gather_scales():
+            for i in range(2):
+                for c in range(chunks):
+                    nc.vector.tensor_copy(slot_planes[i][c][:], planes[i][:].indirect(list_part(c * GATHER, (c + 1) * GATHER)))
+
+        def scale_rows(tiles, o, cols):
+            return tiles[o // 4][4 * (o % 4) : P, cols]
+
+        def load_weights(first, count):
+            raw = raw_pool.tile([P, count, PACK, N], F32, name="raw")
+            rows = w.rearrange("e k n -> (e k) n")[first * K_PASS : (first + count) * K_PASS, :]
+            nc.sync.dma_start(raw[:].rearrange("p g j n -> p g (j n)"), rows.rearrange("(g p j) n -> p g (j n)", p=P, j=PACK))
+            return raw
+
+        def interleave(engine_copy, raw_pass, n0, n1):
+            grouped = grouped_pool.tile([P, n1 - n0, PACK], BF16, name="grouped", align_bytes=64)
+            engine_copy(
+                grouped[:].rearrange("p (c i) j -> p c j i", i=4),
+                raw_pass[:, :, n0:n1].rearrange("p j (c i) -> p c j i", i=4),
+            )
+            return grouped
+
+        def quantize(grouped, label):
+            width = grouped.shape[1]
+            codes = keep.tile([P, width], U32, name="codes" + label, align_bytes=64)
+            scales = keep.tile([P, width], U8, name="scales" + label, align_bytes=64)
+            nc.vector.quantize_mx(out=codes[:].bitcast(FP8X4), scales=scales[:], in_=grouped[:].rearrange("p n j -> p (n j)"))
+            return [(codes[:, c0 : c0 + P], scales[:, c0 : c0 + P]) for c0 in range(0, width, P)]
+
+        banks = {}
+
+        def multiply(e, o, h, operand):
+            codes, scales = operand
+            if e == SHARED:
+                for i, (t0, t1) in enumerate(TOKEN_PIECES):
+                    if o == 0:
+                        banks[e, h, i] = psum.tile([P, t1 - t0], F32, name="acc", tag="shared%d" % (h * len(TOKEN_PIECES) + i))
+                    nc.tensor.matmul_mx(
+                        out=banks[e, h, i][:], lhsT=codes.bitcast(FP8X4), lhsT_scale=scales,
+                        rhs=words[o][:, t0:t1].bitcast(FP8X4), rhs_scale=scale_rows(planes, o, slice(t0, t1)),
+                        start=(o == 0), stop=(o == PASSES - 1),
+                    )
+            else:
+                if o == 0:
+                    banks[e, h] = psum.tile([P, C], F32, name="acc", tag="routed%d" % h)
+                c, j0 = divmod(e * C, GATHER)
+                cols = slice(j0, j0 + C)
+                nc.tensor.matmul_mx(
+                    out=banks[e, h][:], lhsT=codes.bitcast(FP8X4), lhsT_scale=scales,
+                    rhs=slot_words[o][c][:, cols].bitcast(FP8X4),
+                    rhs_scale=scale_rows([slot_planes[0][c], slot_planes[1][c]], o, cols),
+                    start=(o == 0), stop=(o == PASSES - 1),
+                )
+
+        cuts = [0] + list(range(SLOTS - SCATTER * (SLOTS // SCATTER - 1), SLOTS + 1, SCATTER))
+        pending = list(zip(cuts[:-1], cuts[1:]))
+
+        def finish_expert(e):
+            for h in range(HALVES):
+                nc.vector.tensor_scalar(y[h][:, e * C : (e + 1) * C], banks[e, h][:], bias[:, h, e : e + 1], 0.0, ALU.add, ALU.max)
+            for j0, j1 in [cut for cut in pending if cut[1] <= (e + 1) * C]:
+                pending.remove((j0, j1))
+                for h in range(HALVES):
+                    nc.vector.tensor_tensor(routed[h][:].indirect(list_part(j0, j1)), y[h][:, j0:j1], gate_full[:, j0:j1], ALU.mult)
+
+        def finish_shared(h):
+            for i, (t0, t1) in enumerate(TOKEN_PIECES):
+                ys = keep.tile([P, t1 - t0], F32, name="ys%d_%d" % (h, i))
+                nc.scalar.activation(ys[:], banks[SHARED, h, i][:], ACT.Relu, bias=bias[:, h, SHARED : SHARED + 1])
+                total = keep.tile([P, t1 - t0], F32, name="total%d_%d" % (h, i))
+                nc.vector.tensor_tensor(total[:], ys[:], routed[h][:, t0:t1], ALU.add)
+                nc.sync.dma_start(out[h * P : (h + 1) * P, t0:t1], total[:])
+
+        loads = [(0, 1), ("x", 0), (1, 2), ("x", 1), (3, 2), (5, 2), ("x", 2), (7, 2), ("x", 3), (9, 2), (11, 2), ("x", 4)]
+        loads.extend([(g, 2) for g in range(13, 39, 2)])
+        loads.extend([(40, 1), (39, 1), (41, 1), (42, 1), (43, 1), (44, 1)])
+        on_vector = [(3, 1), (5, 1), (7, 1)]
+
+        waiting = []
+        for place, item in enumerate(loads):
+            if 1 <= place <= len(scale_loads):
+                rows, source = scale_loads[place - 1]
+                nc.sync.dma_start(rows.bitcast(I32), source.bitcast(I32))
+                if place == len(scale_loads):
+                    gather_scales()
+            if place == len(scale_loads) + 1:
+                spread_gate()
+            if item[0] == "x":
+                load_tokens(item[1])
+                continue
+            first_pass, count = item
+            raw = load_weights(first_pass, count)
+            for g in range(count):
+                e, o = divmod(first_pass + g, PASSES)
+                if (e, o) == (SHARED, PASSES - 1):
+                    first = interleave(nc.vector.tensor_copy, raw[:, g, :, :], 0, P)
+                    second = interleave(nc.scalar.copy, raw[:, g, :, :], P, N)
+                    operands = quantize(first, "last0") + quantize(second, "last1")
+                else:
+                    copy = nc.vector.tensor_copy if (e, o) in on_vector else nc.scalar.copy
+                    operands = quantize(interleave(copy, raw[:, g, :, :], 0, N), "%d_%d" % (e, o))
+                waiting.append((e, o, operands))
+            if ("x", PASSES - 1) in loads[loads.index(item) :]:
+                continue
+            for e, o, operands in waiting:
+                for h in range(HALVES):
+                    multiply(e, o, h, operands[h])
+                if o == PASSES - 1 and e != SHARED:
+                    finish_expert(e)
+            waiting.clear()
+        for h in range(HALVES):
+            finish_shared(h)

@@ -28,6 +28,8 @@ GATHER = 512
 SCATTER = 160
 BANK = 512
 SHARED = E
+BANKS = 8
+PAIR = 2
 TOKEN_PIECES = [(t0, min(t0 + BANK, T)) for t0 in range(0, T, BANK)]
 
 
@@ -36,7 +38,7 @@ def tile_moe_shr_lin_relu_kernel(tc, x_words, x_scales, w, b, gate, offs, out):
     with ExitStack() as ctx:
         keep = ctx.enter_context(tc.tile_pool(name="keep", bufs=1))
         raw_pool = ctx.enter_context(tc.tile_pool(name="raw", bufs=6))
-        grouped_pool = ctx.enter_context(tc.tile_pool(name="grouped", bufs=8))
+        grouped_pool = ctx.enter_context(tc.tile_pool(name="grouped", bufs=6))
         psum = ctx.enter_context(tc.psum_pool(name="psum", bufs=1))
 
         offsets = keep.tile([P, SLOTS // PER_COLUMN], U16, name="offsets")
@@ -47,23 +49,22 @@ def tile_moe_shr_lin_relu_kernel(tc, x_words, x_scales, w, b, gate, offs, out):
         for plane in planes:
             nc.vector.memset(plane[:].bitcast(I32), 0)
         scale_loads = [(planes[0][32 * q : 32 * q + 16, :], x_scales[0:4, 4 * q : 4 * q + 4, :]) for q in range(4)]
+        identity = keep.tile([P, P], F32, name="identity")
+        make_identity(nc, identity[:])
         scale_loads.extend([(planes[1][32 * q : 32 * q + 4, :], x_scales[4, 4 * q : 4 * q + 4, :]) for q in range(4)])
         bias = keep.tile([P, HALVES, E + 1], F32, name="bias")
 
         routed = [keep.tile([P, T], F32, name="routed%d" % h) for h in range(HALVES)]
         for h in range(HALVES):
             nc.vector.memset(routed[h][:], 0.0)
-        identity = keep.tile([P, P], F32, name="identity")
-        make_identity(nc, identity[:])
 
         gate_full = keep.tile([P, SLOTS], F32, name="gate_full")
         per_bank = BANK // P
 
         def spread_gate():
             nc.sync.dma_start(gate_rows[:], gate[0, :].rearrange("(p m) -> p m", p=P))
-            nc.sync.dma_start(bias[:], b.rearrange("(h p) e -> p h e", p=P))
             for u in range(SLOTS // BANK):
-                turned = psum.tile([P, per_bank, P], F32, name="turned%d" % u, tag="shared%d" % u)
+                turned = psum.tile([P, per_bank, P], F32, name="turned%d" % u, tag="bank%d" % (BANKS - 1 - u))
                 for m in range(per_bank):
                     column = per_bank * u + m
                     nc.tensor.transpose(turned[:, m, :], gate_rows[:, column : column + 1].to_broadcast([P, P]), identity[:])
@@ -73,10 +74,11 @@ def tile_moe_shr_lin_relu_kernel(tc, x_words, x_scales, w, b, gate, offs, out):
                     ACT.Copy,
                 )
 
+        spread_gate()
         words = [keep.tile([P, T], I32, name="words%d" % o, align_bytes=64) for o in range(PASSES)]
         chunks = SLOTS // GATHER
         slot_words = [[keep.tile([P, GATHER], U32, name="slot_words%d_%d" % (o, c), align_bytes=64) for c in range(chunks)] for o in range(PASSES)]
-        slot_planes = [[keep.tile([P, GATHER], U8, name="slot_plane%d_%d" % (i, c), align_bytes=64) for c in range(chunks)] for i in range(2)]
+        slot_planes = [keep.tile([P, SLOTS], U8, name="slot_plane%d" % i, align_bytes=64) for i in range(2)]
         y = [keep.tile([P, SLOTS], F32, name="y%d" % h) for h in range(HALVES)]
 
         def list_part(j0, j1):
@@ -87,10 +89,9 @@ def tile_moe_shr_lin_relu_kernel(tc, x_words, x_scales, w, b, gate, offs, out):
             for c in range(chunks):
                 nc.vector.tensor_copy(slot_words[o][c][:], words[o][:].bitcast(U32).indirect(list_part(c * GATHER, (c + 1) * GATHER)))
 
-        def gather_scales():
-            for i in range(2):
-                for c in range(chunks):
-                    nc.vector.tensor_copy(slot_planes[i][c][:], planes[i][:].indirect(list_part(c * GATHER, (c + 1) * GATHER)))
+        def gather_scales(i):
+            for c in range(chunks):
+                nc.vector.tensor_copy(slot_planes[i][:, c * GATHER : (c + 1) * GATHER], planes[i][:].indirect(list_part(c * GATHER, (c + 1) * GATHER)))
 
         def scale_rows(tiles, o, cols):
             return tiles[o // 4][4 * (o % 4) : P, cols]
@@ -101,29 +102,32 @@ def tile_moe_shr_lin_relu_kernel(tc, x_words, x_scales, w, b, gate, offs, out):
             nc.sync.dma_start(raw[:].rearrange("p g j n -> p g (j n)"), rows.rearrange("(g p j) n -> p g (j n)", p=P, j=PACK))
             return raw
 
-        def interleave(engine_copy, raw_pass, n0, n1):
-            grouped = grouped_pool.tile([P, n1 - n0, PACK], BF16, name="grouped", align_bytes=64)
+        def interleave(engine_copy, raw_part, grouped_part):
             engine_copy(
-                grouped[:].rearrange("p (c i) j -> p c j i", i=4),
-                raw_pass[:, :, n0:n1].rearrange("p j (c i) -> p c j i", i=4),
+                grouped_part.rearrange("p g (c i j) -> p g c j i", i=PAIR, j=PACK),
+                raw_part.rearrange("p g j (c i) -> p g c j i", i=PAIR),
             )
+
+        def ring_tile(count, width):
+            grouped = grouped_pool.tile([P, count, width * PACK], BF16, name="grouped", align_bytes=64)
             return grouped
 
         def quantize(grouped, label):
-            width = grouped.shape[1]
+            width = grouped.shape[1] * grouped.shape[2] // PACK
             codes = keep.tile([P, width], U32, name="codes" + label, align_bytes=64)
             scales = keep.tile([P, width], U8, name="scales" + label, align_bytes=64)
-            nc.vector.quantize_mx(out=codes[:].bitcast(FP8X4), scales=scales[:], in_=grouped[:].rearrange("p n j -> p (n j)"))
+            nc.vector.quantize_mx(out=codes[:].bitcast(FP8X4), scales=scales[:], in_=grouped[:].rearrange("p g c -> p (g c)"))
             return [(codes[:, c0 : c0 + P], scales[:, c0 : c0 + P]) for c0 in range(0, width, P)]
 
         banks = {}
 
-        def multiply(e, o, h, operand):
+        def multiply(e, o, h, operand, pieces=range(len(TOKEN_PIECES))):
             codes, scales = operand
             if e == SHARED:
-                for i, (t0, t1) in enumerate(TOKEN_PIECES):
+                for i in pieces:
+                    t0, t1 = TOKEN_PIECES[i]
                     if o == 0:
-                        banks[e, h, i] = psum.tile([P, t1 - t0], F32, name="acc", tag="shared%d" % (h * len(TOKEN_PIECES) + i))
+                        banks[e, h, i] = psum.tile([P, t1 - t0], F32, name="acc", tag="bank%d" % (h * len(TOKEN_PIECES) + i))
                     nc.tensor.matmul_mx(
                         out=banks[e, h, i][:], lhsT=codes.bitcast(FP8X4), lhsT_scale=scales,
                         rhs=words[o][:, t0:t1].bitcast(FP8X4), rhs_scale=scale_rows(planes, o, slice(t0, t1)),
@@ -131,26 +135,24 @@ def tile_moe_shr_lin_relu_kernel(tc, x_words, x_scales, w, b, gate, offs, out):
                     )
             else:
                 if o == 0:
-                    banks[e, h] = psum.tile([P, C], F32, name="acc", tag="routed%d" % h)
+                    banks[e, h] = psum.tile([P, C], F32, name="acc", tag="bank%d" % (HALVES * (e % 4 if e < 5 else 3) + h))
                 c, j0 = divmod(e * C, GATHER)
                 cols = slice(j0, j0 + C)
                 nc.tensor.matmul_mx(
                     out=banks[e, h][:], lhsT=codes.bitcast(FP8X4), lhsT_scale=scales,
                     rhs=slot_words[o][c][:, cols].bitcast(FP8X4),
-                    rhs_scale=scale_rows([slot_planes[0][c], slot_planes[1][c]], o, cols),
+                    rhs_scale=scale_rows(slot_planes, o, slice(e * C, (e + 1) * C)),
                     start=(o == 0), stop=(o == PASSES - 1),
                 )
 
         cuts = [0] + list(range(SLOTS - SCATTER * (SLOTS // SCATTER - 1), SLOTS + 1, SCATTER))
-        pending = list(zip(cuts[:-1], cuts[1:]))
+        pending = [list(zip(cuts[:-1], cuts[1:])) for h in range(HALVES)]
 
-        def finish_expert(e):
-            for h in range(HALVES):
-                nc.vector.tensor_scalar(y[h][:, e * C : (e + 1) * C], banks[e, h][:], bias[:, h, e : e + 1], 0.0, ALU.add, ALU.max)
-            for j0, j1 in [cut for cut in pending if cut[1] <= (e + 1) * C]:
-                pending.remove((j0, j1))
-                for h in range(HALVES):
-                    nc.vector.tensor_tensor(routed[h][:].indirect(list_part(j0, j1)), y[h][:, j0:j1], gate_full[:, j0:j1], ALU.mult)
+        def finish_expert(e, h):
+            nc.vector.tensor_scalar(y[h][:, e * C : (e + 1) * C], banks[e, h][:], bias[:, h, e : e + 1], 0.0, ALU.add, ALU.max)
+            for j0, j1 in [cut for cut in pending[h] if cut[1] <= (e + 1) * C]:
+                pending[h].remove((j0, j1))
+                nc.vector.tensor_tensor(routed[h][:].indirect(list_part(j0, j1)), y[h][:, j0:j1], gate_full[:, j0:j1], ALU.mult)
 
         def finish_shared(h):
             for i, (t0, t1) in enumerate(TOKEN_PIECES):
@@ -160,42 +162,70 @@ def tile_moe_shr_lin_relu_kernel(tc, x_words, x_scales, w, b, gate, offs, out):
                 nc.vector.tensor_tensor(total[:], ys[:], routed[h][:, t0:t1], ALU.add)
                 nc.sync.dma_start(out[h * P : (h + 1) * P, t0:t1], total[:])
 
-        loads = [(0, 1), ("x", 0), (1, 2), ("x", 1), (3, 2), (5, 2), ("x", 2), (7, 2), ("x", 3), (9, 2), (11, 2), ("x", 4)]
-        loads.extend([(g, 2) for g in range(13, 39, 2)])
-        loads.extend([(40, 1), (39, 1), (41, 1), (42, 1), (43, 1), (44, 1)])
-        on_vector = [(3, 1), (5, 1), (7, 1)]
+        loads = [("x", 0), (0, 1), (1, 2), ("x", 1), (3, 2), ("x", 2), (5, 2), ("x", 3), (7, 2), (9, 2), ("x", 4)]
+        loads.extend([(g, 2) for g in range(11, 35, 2)])
+        loads.extend([(35, 2), (40, 1), (37, 2), (41, 1)])
+        on_vector = [19, 25]
 
         waiting = []
         for place, item in enumerate(loads):
-            if 1 <= place <= len(scale_loads):
-                rows, source = scale_loads[place - 1]
-                nc.sync.dma_start(rows.bitcast(I32), source.bitcast(I32))
-                if place == len(scale_loads):
-                    gather_scales()
-            if place == len(scale_loads) + 1:
-                spread_gate()
+            if 1 <= place <= 4:
+                for rows, source in scale_loads[2 * place - 2 : 2 * place]:
+                    nc.sync.dma_start(rows.bitcast(I32), source.bitcast(I32))
+                if place % 2 == 0:
+                    gather_scales(place // 2 - 1)
+            if place == 5:
+                nc.sync.dma_start(bias[:], b.rearrange("(h p) e -> p h e", p=P))
             if item[0] == "x":
                 load_tokens(item[1])
                 continue
             first_pass, count = item
             raw = load_weights(first_pass, count)
-            for g in range(count):
-                e, o = divmod(first_pass + g, PASSES)
-                if (e, o) == (SHARED, PASSES - 1):
-                    first = interleave(nc.vector.tensor_copy, raw[:, g, :, :], 0, P)
-                    second = interleave(nc.scalar.copy, raw[:, g, :, :], P, N)
-                    operands = quantize(first, "last0") + quantize(second, "last1")
-                else:
-                    copy = nc.vector.tensor_copy if (e, o) in on_vector else nc.scalar.copy
-                    operands = quantize(interleave(copy, raw[:, g, :, :], 0, N), "%d_%d" % (e, o))
-                waiting.append((e, o, operands))
-            if ("x", PASSES - 1) in loads[loads.index(item) :]:
+            grouped = ring_tile(count, N)
+            if first_pass in on_vector:
+                interleave(nc.vector.tensor_copy, raw[:, 0:1, :, :], grouped[:, 0:1, :])
+                interleave(nc.scalar.copy, raw[:, 1:2, :, :], grouped[:, 1:2, :])
+            else:
+                interleave(nc.scalar.copy, raw[:], grouped[:])
+            operands = quantize(grouped, "%d" % first_pass)
+            waiting.extend([(first_pass + g, operands[HALVES * g : HALVES * (g + 1)]) for g in range(count)])
+            if ("x", PASSES - 1) in loads[place:]:
                 continue
-            for e, o, operands in waiting:
+            for flat, operands in waiting:
+                e, o = divmod(flat, PASSES)
                 for h in range(HALVES):
                     multiply(e, o, h, operands[h])
                 if o == PASSES - 1 and e != SHARED:
-                    finish_expert(e)
+                    for h in range(HALVES):
+                        finish_expert(e, h)
             waiting.clear()
+
+        raws = {}
+
+        def by_halves(parts):
+            grouped = ring_tile(len(parts), P)
+            for g, (flat, h) in enumerate(parts):
+                if flat not in raws:
+                    raws[flat] = load_weights(flat, 1)
+                interleave(nc.scalar.copy, raws[flat][:, :, :, h * P : (h + 1) * P], grouped[:, g : g + 1, :])
+            return quantize(grouped, "end%d_%d" % parts[0])
+
+        a, = by_halves([(39, 0)])
+        multiply(E - 1, PASSES - 1, 0, a)
+        a, = by_halves([(42, 0)])
+        multiply(SHARED, 2, 0, a)
+        finish_expert(E - 1, 0)
+        a, c = by_halves([(39, 1), (42, 1)])
+        multiply(E - 1, PASSES - 1, 1, a)
+        multiply(SHARED, 2, 1, c)
+        a, = by_halves([(43, 0)])
+        multiply(SHARED, 3, 0, a)
+        finish_expert(E - 1, 1)
+        a, = by_halves([(44, 0)])
+        multiply(SHARED, 4, 0, a)
+        a, c = by_halves([(43, 1), (44, 1)])
+        for piece in range(len(TOKEN_PIECES)):
+            multiply(SHARED, 3, 1, a, [piece])
+            multiply(SHARED, 4, 1, c, [piece])
         for h in range(HALVES):
             finish_shared(h)

from contextlib import ExitStack

import concourse.mybir as mybir
from concourse.masks import make_identity

K, T, E, C, N = 2560, 1280, 8, 128, 256
SLOTS = E * C
FLOPS = 2 * K * N * (SLOTS + T)
BYTES = K * T + K * T // 32 + (E + 1) * K * N * 4 + N * (E + 1) * 4 + SLOTS * 4 + 128 * (SLOTS // 16) * 2 + N * T * 4

F32 = mybir.dt.float32
BF16 = mybir.dt.bfloat16
I32 = mybir.dt.int32
U32 = mybir.dt.uint32
U16 = mybir.dt.uint16
U8 = mybir.dt.uint8
FP8X4 = mybir.dt.float8_e4m3fn_x4
ALU = mybir.AluOpType
ACT = mybir.ActivationFunctionType

P = 128
PACK = 4
K_PASS = P * PACK
PASSES = K // K_PASS
HALVES = N // P
PER_COLUMN = 16
GATHER = 512
SCATTER = 160
BANK = 512
SHARED = E
BANKS = 8
PAIR = 2
TOKEN_PIECES = [(t0, min(t0 + BANK, T)) for t0 in range(0, T, BANK)]


def tile_moe_shr_lin_relu_kernel(tc, x_words, x_scales, w, b, gate, offs, out):
    nc = tc.nc
    with ExitStack() as ctx:
        keep = ctx.enter_context(tc.tile_pool(name="keep", bufs=1))
        raw_pool = ctx.enter_context(tc.tile_pool(name="raw", bufs=6))
        grouped_pool = ctx.enter_context(tc.tile_pool(name="grouped", bufs=6))
        psum = ctx.enter_context(tc.psum_pool(name="psum", bufs=1))

        offsets = keep.tile([P, SLOTS // PER_COLUMN], U16, name="offsets")
        nc.sync.dma_start(offsets[:], offs)

        gate_rows = keep.tile([P, SLOTS // P], F32, name="gate_rows")
        planes = [keep.tile([P, T], U8, name="plane%d" % i, align_bytes=64) for i in range(2)]
        for plane in planes:
            nc.vector.memset(plane[:].bitcast(I32), 0)
        scale_loads = [(planes[0][32 * q : 32 * q + 16, :], x_scales[0:4, 4 * q : 4 * q + 4, :]) for q in range(4)]
        identity = keep.tile([P, P], F32, name="identity")
        make_identity(nc, identity[:])
        scale_loads.extend([(planes[1][32 * q : 32 * q + 4, :], x_scales[4, 4 * q : 4 * q + 4, :]) for q in range(4)])
        bias = keep.tile([P, HALVES, E + 1], F32, name="bias")

        routed = [keep.tile([P, T], F32, name="routed%d" % h) for h in range(HALVES)]
        for h in range(HALVES):
            nc.vector.memset(routed[h][:], 0.0)

        gate_full = keep.tile([P, SLOTS], F32, name="gate_full")
        per_bank = BANK // P

        def spread_gate():
            nc.sync.dma_start(gate_rows[:], gate[0, :].rearrange("(p m) -> p m", p=P))
            for u in range(SLOTS // BANK):
                turned = psum.tile([P, per_bank, P], F32, name="turned%d" % u, tag="bank%d" % (BANKS - 1 - u))
                for m in range(per_bank):
                    column = per_bank * u + m
                    nc.tensor.transpose(turned[:, m, :], gate_rows[:, column : column + 1].to_broadcast([P, P]), identity[:])
                nc.scalar.activation(
                    gate_full[:].rearrange("q (p m) -> q p m", p=P)[:, :, per_bank * u : per_bank * (u + 1)],
                    turned[:].rearrange("q m p -> q p m"),
                    ACT.Copy,
                )

        spread_gate()
        words = [keep.tile([P, T], I32, name="words%d" % o, align_bytes=64) for o in range(PASSES)]
        chunks = SLOTS // GATHER
        slot_words = [[keep.tile([P, GATHER], U32, name="slot_words%d_%d" % (o, c), align_bytes=64) for c in range(chunks)] for o in range(PASSES)]
        slot_planes = [keep.tile([P, SLOTS], U8, name="slot_plane%d" % i, align_bytes=64) for i in range(2)]
        y = [keep.tile([P, SLOTS], F32, name="y%d" % h) for h in range(HALVES)]

        def list_part(j0, j1):
            return offsets[:, j0 // PER_COLUMN : j1 // PER_COLUMN]

        def load_tokens(o):
            nc.sync.dma_start(words[o][:], x_words[o].rearrange("p t r -> p (t r)").bitcast(I32))
            for c in range(chunks):
                nc.vector.tensor_copy(slot_words[o][c][:], words[o][:].bitcast(U32).indirect(list_part(c * GATHER, (c + 1) * GATHER)))

        def gather_scales(i):
            for c in range(chunks):
                nc.vector.tensor_copy(slot_planes[i][:, c * GATHER : (c + 1) * GATHER], planes[i][:].indirect(list_part(c * GATHER, (c + 1) * GATHER)))

        def scale_rows(tiles, o, cols):
            return tiles[o // 4][4 * (o % 4) : P, cols]

        def load_weights(first, count):
            raw = raw_pool.tile([P, count, PACK, N], F32, name="raw")
            rows = w.rearrange("e k n -> (e k) n")[first * K_PASS : (first + count) * K_PASS, :]
            nc.sync.dma_start(raw[:].rearrange("p g j n -> p g (j n)"), rows.rearrange("(g p j) n -> p g (j n)", p=P, j=PACK))
            return raw

        def interleave(engine_copy, raw_part, grouped_part):
            engine_copy(
                grouped_part.rearrange("p g (c i j) -> p g c j i", i=PAIR, j=PACK),
                raw_part.rearrange("p g j (c i) -> p g c j i", i=PAIR),
            )

        def ring_tile(count, width):
            grouped = grouped_pool.tile([P, count, width * PACK], BF16, name="grouped", align_bytes=64)
            return grouped

        def quantize(grouped, label):
            width = grouped.shape[1] * grouped.shape[2] // PACK
            codes = keep.tile([P, width], U32, name="codes" + label, align_bytes=64)
            scales = keep.tile([P, width], U8, name="scales" + label, align_bytes=64)
            nc.vector.quantize_mx(out=codes[:].bitcast(FP8X4), scales=scales[:], in_=grouped[:].rearrange("p g c -> p (g c)"))
            return [(codes[:, c0 : c0 + P], scales[:, c0 : c0 + P]) for c0 in range(0, width, P)]

        banks = {}

        def multiply(e, o, h, operand, pieces=range(len(TOKEN_PIECES))):
            codes, scales = operand
            if e == SHARED:
                for i in pieces:
                    t0, t1 = TOKEN_PIECES[i]
                    if o == 0:
                        banks[e, h, i] = psum.tile([P, t1 - t0], F32, name="acc", tag="bank%d" % (h * len(TOKEN_PIECES) + i))
                    nc.tensor.matmul_mx(
                        out=banks[e, h, i][:], lhsT=codes.bitcast(FP8X4), lhsT_scale=scales,
                        rhs=words[o][:, t0:t1].bitcast(FP8X4), rhs_scale=scale_rows(planes, o, slice(t0, t1)),
                        start=(o == 0), stop=(o == PASSES - 1),
                    )
            else:
                if o == 0:
                    banks[e, h] = psum.tile([P, C], F32, name="acc", tag="bank%d" % (HALVES * (e % 4 if e < 5 else 3) + h))
                c, j0 = divmod(e * C, GATHER)
                cols = slice(j0, j0 + C)
                nc.tensor.matmul_mx(
                    out=banks[e, h][:], lhsT=codes.bitcast(FP8X4), lhsT_scale=scales,
                    rhs=slot_words[o][c][:, cols].bitcast(FP8X4),
                    rhs_scale=scale_rows(slot_planes, o, slice(e * C, (e + 1) * C)),
                    start=(o == 0), stop=(o == PASSES - 1),
                )

        cuts = [0] + list(range(SLOTS - SCATTER * (SLOTS // SCATTER - 1), SLOTS + 1, SCATTER))
        pending = [list(zip(cuts[:-1], cuts[1:])) for h in range(HALVES)]

        def finish_expert(e, h):
            nc.vector.tensor_scalar(y[h][:, e * C : (e + 1) * C], banks[e, h][:], bias[:, h, e : e + 1], 0.0, ALU.add, ALU.max)
            for j0, j1 in [cut for cut in pending[h] if cut[1] <= (e + 1) * C]:
                pending[h].remove((j0, j1))
                nc.vector.tensor_tensor(routed[h][:].indirect(list_part(j0, j1)), y[h][:, j0:j1], gate_full[:, j0:j1], ALU.mult)

        def finish_shared(h):
            for i, (t0, t1) in enumerate(TOKEN_PIECES):
                ys = keep.tile([P, t1 - t0], F32, name="ys%d_%d" % (h, i))
                nc.scalar.activation(ys[:], banks[SHARED, h, i][:], ACT.Relu, bias=bias[:, h, SHARED : SHARED + 1])
                total = keep.tile([P, t1 - t0], F32, name="total%d_%d" % (h, i))
                nc.vector.tensor_tensor(total[:], ys[:], routed[h][:, t0:t1], ALU.add)
                nc.sync.dma_start(out[h * P : (h + 1) * P, t0:t1], total[:])

        loads = [("x", 0), (0, 1), (1, 2), ("x", 1), (3, 2), ("x", 2), (5, 2), ("x", 3), (7, 2), (9, 2), ("x", 4)]
        loads.extend([(g, 2) for g in range(11, 35, 2)])
        loads.extend([(35, 2), (40, 1), (37, 2), (41, 1)])
        on_vector = [19, 25]

        waiting = []
        for place, item in enumerate(loads):
            if 1 <= place <= 4:
                for rows, source in scale_loads[2 * place - 2 : 2 * place]:
                    nc.sync.dma_start(rows.bitcast(I32), source.bitcast(I32))
                if place % 2 == 0:
                    gather_scales(place // 2 - 1)
            if place == 5:
                nc.sync.dma_start(bias[:], b.rearrange("(h p) e -> p h e", p=P))
            if item[0] == "x":
                load_tokens(item[1])
                continue
            first_pass, count = item
            raw = load_weights(first_pass, count)
            grouped = ring_tile(count, N)
            if first_pass in on_vector:
                interleave(nc.vector.tensor_copy, raw[:, 0:1, :, :], grouped[:, 0:1, :])
                interleave(nc.scalar.copy, raw[:, 1:2, :, :], grouped[:, 1:2, :])
            else:
                interleave(nc.scalar.copy, raw[:], grouped[:])
            operands = quantize(grouped, "%d" % first_pass)
            waiting.extend([(first_pass + g, operands[HALVES * g : HALVES * (g + 1)]) for g in range(count)])
            if ("x", PASSES - 1) in loads[place:]:
                continue
            for flat, operands in waiting:
                e, o = divmod(flat, PASSES)
                for h in range(HALVES):
                    multiply(e, o, h, operands[h])
                if o == PASSES - 1 and e != SHARED:
                    for h in range(HALVES):
                        finish_expert(e, h)
            waiting.clear()

        raws = {}

        def by_halves(parts):
            grouped = ring_tile(len(parts), P)
            for g, (flat, h) in enumerate(parts):
                if flat not in raws:
                    raws[flat] = load_weights(flat, 1)
                interleave(nc.scalar.copy, raws[flat][:, :, :, h * P : (h + 1) * P], grouped[:, g : g + 1, :])
            return quantize(grouped, "end%d_%d" % parts[0])

        a, = by_halves([(39, 0)])
        multiply(E - 1, PASSES - 1, 0, a)
        a, = by_halves([(42, 0)])
        multiply(SHARED, 2, 0, a)
        finish_expert(E - 1, 0)
        a, c = by_halves([(39, 1), (42, 1)])
        multiply(E - 1, PASSES - 1, 1, a)
        multiply(SHARED, 2, 1, c)
        a, = by_halves([(43, 0)])
        multiply(SHARED, 3, 0, a)
        finish_expert(E - 1, 1)
        a, = by_halves([(44, 0)])
        multiply(SHARED, 4, 0, a)
        a, c = by_halves([(43, 1), (44, 1)])
        for piece in range(len(TOKEN_PIECES)):
            multiply(SHARED, 3, 1, a, [piece])
            multiply(SHARED, 4, 1, c, [piece])
        for h in range(HALVES):
            finish_shared(h)
